import numpy as np
import ml_dtypes


def mxq(x, axis, fmt="e4m3"):
    dtype, down = {"e4m3": (ml_dtypes.float8_e4m3fn, 7), "e5m2": (ml_dtypes.float8_e5m2, 14)}[fmt]
    v = np.moveaxis(np.asarray(x, np.float32).astype(ml_dtypes.bfloat16).astype(np.float64), axis, -1)
    blocks = v.reshape(v.shape[:-1] + (-1, 32))
    amax = np.abs(blocks).max(-1, keepdims=True)
    byte = np.maximum(np.where(amax > 0, np.frexp(amax)[1] - 1 + 127, 0) - down, 1)
    scale = np.exp2(byte - 127.0)
    codes = (blocks / scale).astype(np.float32).astype(dtype).astype(np.float64)
    return np.moveaxis((codes * scale).reshape(v.shape), -1, axis)


WIDE = False


def mx_kscale(k):
    if not WIDE:
        return np.ones(k)
    levels = np.array([10, -10, 5, -5, 0])
    if k % 512:
        return np.exp2(np.random.permutation(np.resize(levels, k // 32))).repeat(32)
    a = np.empty((k // 512, 16))
    for p in range(k // 512):
        a[p, :8] = np.random.permutation(np.resize(levels, 8))
        for g in range(8):
            far = levels[np.abs(levels - a[p, g]) >= 10]
            a[p, g + 8] = far[np.random.randint(len(far))]
    return np.exp2(a.ravel()).repeat(32)


def f64(x):
    return np.asarray(x).astype(np.float64)


def striped(idx):
    return np.tile(np.asarray(idx).reshape(-1, 16).T, (8, 1)).astype(np.uint16)


def unstriped(offs):
    return offs[:16].T.reshape(-1).astype(np.int64)


E2M1 = np.array([0.0, 0.5, 1.0, 1.5, 2.0, 3.0, 4.0, 6.0, -0.0, -0.5, -1.0, -1.5, -2.0, -3.0, -4.0, -6.0])


def pack_weight(w, fmt):
    k, n = w.shape
    w = f64(np.asarray(w, np.float32).astype(ml_dtypes.bfloat16)).reshape(k // 32, 32, n)
    amax = np.abs(w).max(1)
    if fmt == "e4m3":
        byte = np.frexp(amax)[1] - 1 + 127 - 7
    else:
        mant, ex = np.frexp(amax / 6.0)
        byte = np.where(mant > 0.5, ex, ex - 1) + 127
    byte = np.clip(np.where(amax > 0, byte, 1), 1, 254)
    scaled = (w * np.exp2(127.0 - byte)[:, None, :]).reshape(k, n).astype(np.float32)
    by_word = np.ascontiguousarray(scaled.reshape(k // 512, 128, 4, n).transpose(0, 1, 3, 2))
    if fmt == "e4m3":
        words = by_word.astype(ml_dtypes.float8_e4m3fn).view(np.uint8)
    else:
        c = by_word.astype(ml_dtypes.float4_e2m1fn).view(np.uint8) & 0xF
        words = (c[..., 0::2] | (c[..., 1::2] << 4)).reshape(k // 512, 128, 2 * n)
    return np.ascontiguousarray(words), np.ascontiguousarray(byte.astype(np.uint8).reshape(k // 512, 16, n))


def unpack_weight(words, scales, fmt):
    g, _, n = scales.shape
    words = np.ascontiguousarray(words).reshape(g, 128, n, -1)
    if fmt == "e4m3":
        vals = words.view(ml_dtypes.float8_e4m3fn).astype(np.float64)
    else:
        nib = np.empty((g, 128, n, 4), np.uint8)
        nib[..., 0::2] = words & 0xF
        nib[..., 1::2] = words >> 4
        vals = E2M1[nib]
    vals = vals * np.repeat(np.exp2(scales.astype(np.float64) - 127.0), 8, axis=1)[..., None]
    return vals.transpose(0, 1, 3, 2).reshape(g * 512, n)


D, T, I, J, U, Z, E, M, C = 512, 2048, 512, 256, 1024, 1024, 512, 1024, 512


def setup_inputs():
    n = np.random.standard_normal
    idx = np.random.permutation(T)[:I]
    idx2 = np.random.permutation(U)[:J]
    idx3 = np.random.permutation(Z)[:J]
    idx4 = np.random.permutation(M)[:J]
    fd = mx_kscale(D)
    fi = mx_kscale(I)
    fc = mx_kscale(C)
    ti = np.ones(T)
    ti[idx] = fi
    keysp = pack_weight(n((D, T)) / fd[:, None], "e4m3")
    return {
        "keys_words": keysp[0],
        "keys_scales": keysp[1],
        "notes": (n((D, U)) * 1.0 / np.sqrt(D) * fd[:, None]).astype(np.float32),
        "users2": (n((D, Z)) * 1.0 / np.sqrt(D) * fd[:, None]).astype(np.float32),
        "rowf": (np.random.uniform(0.02, 0.08, (I, 1)) * fi[:, None]).astype(np.float32),
        "vals": (n((E, T)) / ti).astype(np.float32),
        "wm": (n((C, E)) * 1.0 / np.sqrt(C) * fc[:, None]).astype(np.float32),
        "mstore": (n((C, M)) / fc[:, None]).astype(np.float32),
        "offs": striped(idx),
        "offs2": striped(idx2),
        "offs3": striped(idx3),
        "offs4": striped(idx4),
    }


def reference(keys_words, keys_scales, notes, users2, rowf, vals, wm, mstore, offs, offs2, offs3, offs4):
    idx = unstriped(offs)
    idx2 = unstriped(offs2)
    idx3 = unstriped(offs3)
    idx4 = unstriped(offs4)
    keysu = unpack_weight(keys_words, keys_scales, "e4m3")
    keysidxg = keysu[:, idx]
    notesidx2q = mxq(f64(notes)[:, idx2], 0, "e4m3")
    g1 = keysidxg.T @ notesidx2q
    users2idx3q = mxq(f64(users2)[:, idx3], 0, "e4m3")
    g2 = keysidxg.T @ users2idx3q
    g0 = np.maximum(g1, g2)
    gr1 = g0 * f64(rowf)
    vt1 = f64(vals)[:, idx].T
    vt1q = mxq(vt1, 0, "e4m3")
    gr1q = mxq(gr1, 0, "e4m3")
    o = vt1q.T @ gr1q
    wmq = mxq(f64(wm), 0, "e4m3")
    mstoreq = mxq(f64(mstore), 0, "e4m3")
    me = wmq.T @ mstoreq
    y = o * me[:, idx4]
    return y

@@ -1,0 +1,229 @@
+from contextlib import ExitStack
+
+import concourse.mybir as mybir
+from concourse.masks import make_identity
+
+D, T, I, J, U, Z, E, M, C = 512, 2048, 512, 256, 1024, 1024, 512, 1024, 512
+FLOPS = 2 * (2 * D * I * J + I * E * J + C * E * M)
+
+F32 = mybir.dt.float32
+BF16 = mybir.dt.bfloat16
+I32 = mybir.dt.int32
+U32 = mybir.dt.uint32
+U16 = mybir.dt.uint16
+U8 = mybir.dt.uint8
+FP8X4 = mybir.dt.float8_e4m3fn_x4
+COPY = mybir.ActivationFunctionType.Copy
+MULT = mybir.AluOpType.mult
+MAX = mybir.AluOpType.max
+
+P = 128
+PACK = 4
+BANK = 512
+E_BLOCKS = E // P
+M_HALVES = M // BANK
+J_HALVES = J // P
+
+
+def interleave(nc, woven, planes):
+    nc.vector.tensor_copy(
+        out=woven.rearrange("p (c i) t -> p c t i", i=4),
+        in_=planes.rearrange("p t (c i) -> p c t i", i=4),
+    )
+
+
+def quantize(nc, pool, woven, name):
+    width = woven.shape[1]
+    codes = pool.tile([P, width], U32, name=name + "_codes", align_bytes=64)
+    scales = pool.tile([P, width], U8, name=name + "_scales", align_bytes=64)
+    nc.vector.quantize_mx(out=codes[:].bitcast(FP8X4), scales=scales[:], in_=woven.rearrange("p w t -> p (w t)"))
+    return codes, scales
+
+
+def multiply(nc, out, left, left_cols, right, right_cols):
+    nc.tensor.matmul_mx(
+        out=out,
+        lhsT=left[0][:, left_cols].bitcast(FP8X4),
+        lhsT_scale=left[1][:, left_cols],
+        rhs=right[0][:, right_cols].bitcast(FP8X4),
+        rhs_scale=right[1][:, right_cols],
+        start=True,
+        stop=True,
+    )
+
+
+def cols(n, width):
+    return slice(n * width, (n + 1) * width)
+
+
+def tile_attend_tab_larger_gains_kernel(
+    tc, keys_words, keys_scales, notes, users2, rowf, vals, wm, mstore, offs, offs2, offs3, offs4, out
+):
+    nc = tc.nc
+    with ExitStack() as ctx:
+        lists = ctx.enter_context(tc.tile_pool(name="lists", bufs=1))
+        sb = ctx.enter_context(tc.tile_pool(name="sb", bufs=1))
+        psum = ctx.enter_context(tc.psum_pool(name="psum", bufs=1))
+
+        def load_list(src, name):
+            tile = lists.tile(list(src.shape), U16, name=name)
+            nc.sync.dma_start(tile[:], src)
+            return tile
+
+        def load_plane_pairs(src, name):
+            rows = src.rearrange("(p t) n -> p t n", t=PACK)
+            pairs = []
+            for a in range(2):
+                pair = sb.tile([P, 2, src.shape[1]], F32, name=name + str(a))
+                nc.sync.dma_start(out=pair[:], in_=rows[:, 2 * a : 2 * a + 2, :])
+                pairs.append(pair)
+            return pairs
+
+        key_scales = sb.tile([P, T], U8)
+        nc.vector.memset(key_scales[:].bitcast(I32), 0)
+        wm_raw = sb.tile([P, PACK, E], F32)
+        nc.sync.dma_start(out=wm_raw[:], in_=wm.rearrange("(p t) e -> p t e", t=PACK))
+        for q in range(4):
+            nc.sync.dma_start(
+                out=key_scales[32 * q : 32 * q + 4, :].bitcast(I32),
+                in_=keys_scales[0, 4 * q : 4 * q + 4, :].bitcast(I32),
+            )
+        mstore_rows = mstore.rearrange("(p t) m -> p t m", t=PACK)
+        mstore_raw = []
+        for h in range(M_HALVES):
+            half = sb.tile([P, PACK, BANK], F32, name="mstore_raw" + str(h))
+            nc.sync.dma_start(out=half[:], in_=mstore_rows[:, :, cols(h, BANK)])
+            mstore_raw.append(half)
+        key_words = sb.tile([P, T], U32)
+        nc.sync.dma_start(
+            out=key_words[:].bitcast(I32), in_=keys_words[0].rearrange("p n t -> p (n t)").bitcast(I32)
+        )
+        token_list = load_list(offs, "token_list")
+        memory_list = load_list(offs4, "memory_list")
+        note_list = load_list(offs2, "note_list")
+        user_list = load_list(offs3, "user_list")
+        row_factors = sb.tile([P, PACK], F32)
+        nc.sync.dma_start(out=row_factors[:], in_=rowf.rearrange("(p t) o -> p (t o)", t=PACK))
+        note_pairs = load_plane_pairs(notes, "note_pair")
+        user_rows = users2.rearrange("(p t) n -> p t n", t=PACK)
+        user_pair = sb.tile([P, 2, Z], F32)
+        nc.sync.dma_start(out=user_pair[:], in_=user_rows[:, 0:2, :])
+        user_singles = []
+        for t in (2, 3):
+            single = sb.tile([P, Z], F32, name="user_single" + str(t))
+            nc.sync.dma_start(out=single[:], in_=user_rows[:, t, :])
+            user_singles.append(single)
+        val_blocks = []
+        for b in range(E_BLOCKS):
+            block = sb.tile([P, T], F32, name="val_block" + str(b), tag="val_block" + str(b))
+            nc.sync.dma_start(out=block[:], in_=vals[cols(b, P), :])
+            val_blocks.append(block)
+
+        identity = sb.tile([P, P], F32)
+        make_identity(nc, identity[:])
+
+        wm_woven = sb.tile([P, E, PACK], BF16, align_bytes=64)
+        interleave(nc, wm_woven[:], wm_raw[:])
+        wm_q = quantize(nc, sb, wm_woven[:], "wm")
+        memories = [sb.tile([P, M], F32, name="memories" + str(b)) for b in range(E_BLOCKS)]
+        for h in range(M_HALVES):
+            mstore_woven = sb.tile([P, BANK, PACK], BF16, name="mstore_woven" + str(h), align_bytes=64)
+            interleave(nc, mstore_woven[:], mstore_raw[h][:])
+            mstore_q = quantize(nc, sb, mstore_woven[:], "mstore" + str(h))
+            for b in range(E_BLOCKS):
+                memory_bank = psum.tile([P, BANK], F32, bufs=3)
+                multiply(nc, memory_bank[:], wm_q, cols(b, P), mstore_q, cols(0, BANK))
+                nc.scalar.copy(out=memories[b][:, cols(h, BANK)], in_=memory_bank[:])
+        picked_memories = []
+        for b in range(E_BLOCKS):
+            picked = sb.tile([P, J], F32, name="picked_memories" + str(b))
+            nc.scalar.activation(picked[:], memories[b][:].indirect(memory_list[:]), COPY)
+            picked_memories.append(picked)
+
+        picked_words = sb.tile([P, I], U32, align_bytes=64)
+        nc.vector.tensor_copy(
+            picked_words[:].rearrange("p (t s) -> p s t", t=PACK), key_words[:].indirect(token_list[:])
+        )
+        picked_scales = sb.tile([P, I], U8, align_bytes=64)
+        nc.vector.tensor_copy(
+            picked_scales[:].rearrange("p (t s) -> p s t", t=PACK), key_scales[:].indirect(token_list[:])
+        )
+        keys_q = (picked_words, picked_scales)
+
+        def table_half(columns_q, columns):
+            table_bank = psum.tile([P, PACK, P], F32, bufs=2)
+            for t in range(PACK):
+                multiply(nc, table_bank[:, t, :], keys_q, cols(t, P), columns_q, columns)
+            return table_bank[:].rearrange("p t j -> p j t")
+
+        note_planes = sb.tile([P, PACK, J], F32)
+        for t in range(PACK):
+            nc.vector.tensor_copy(note_planes[:, t, :], note_pairs[t // 2][:, t % 2, :].indirect(note_list[:]))
+        notes_woven = sb.tile([P, J, PACK], BF16, align_bytes=64)
+        interleave(nc, notes_woven[:], note_planes[:])
+        notes_q = quantize(nc, sb, notes_woven[:], "notes")
+        g1 = sb.tile([P, J, PACK], F32)
+        for h in range(J_HALVES):
+            nc.scalar.copy(out=g1[:, cols(h, P), :], in_=table_half(notes_q, cols(h, P)))
+
+        user_planes = sb.tile([P, PACK, J], F32)
+        nc.vector.tensor_copy(user_planes[:, 0, :], user_pair[:, 0, :].indirect(user_list[:]))
+        nc.scalar.activation(user_planes[:, 1, :], user_pair[:, 1, :].indirect(user_list[:]), COPY)
+        nc.vector.tensor_copy(user_planes[:, 2, :], user_singles[0][:].indirect(user_list[:]))
+        nc.vector.tensor_copy(user_planes[:, 3, :P], user_singles[1][:].indirect(user_list[:, : P // 16]))
+        nc.scalar.activation(user_planes[:, 3, P:], user_singles[1][:].indirect(user_list[:, P // 16 :]), COPY)
+        users_woven = [sb.tile([P, P, PACK], BF16, name="users_woven" + str(h), align_bytes=64) for h in range(J_HALVES)]
+        for h in range(J_HALVES):
+            interleave(nc, users_woven[h][:], user_planes[:, :, cols(h, P)])
+        users_q = [quantize(nc, sb, users_woven[h][:], "users" + str(h)) for h in range(J_HALVES)]
+        g0 = sb.tile([P, J, PACK], F32)
+        gr1 = sb.tile([P, J, PACK], BF16, align_bytes=64)
+        for h in range(J_HALVES):
+            nc.vector.tensor_tensor(
+                g0[:, cols(h, P), :], table_half(users_q[h], cols(0, P)), g1[:, cols(h, P), :], MAX
+            )
+        for h in range(J_HALVES):
+            nc.vector.tensor_tensor(
+                gr1[:, cols(h, P), :],
+                g0[:, cols(h, P), :],
+                row_factors[:].unsqueeze(1).to_broadcast([P, P, PACK]),
+                MULT,
+            )
+        gr1_q = quantize(nc, sb, gr1[:], "gr1")
+
+        list_cols = I // 16
+
+        def prepare(b, bank):
+            picked_vals = sb.tile([P, I], BF16, name="picked_vals" + str(b))
+            if b < E_BLOCKS - 1:
+                nc.scalar.activation(picked_vals[:], val_blocks[b][:].indirect(token_list[:]), COPY)
+            else:
+                nc.scalar.activation(
+                    picked_vals[:, : I // 2], val_blocks[b][:].indirect(token_list[:, : list_cols // 2]), COPY
+                )
+                nc.vector.tensor_copy(
+                    picked_vals[:, I // 2 :], val_blocks[b][:].indirect(token_list[:, list_cols // 2 :])
+                )
+            pair_words = picked_vals[:].bitcast(F32)
+            turned = psum.tile([P, 2, P], F32, tag=bank)
+            for u in range(2):
+                nc.tensor.transpose(turned[:, u, :], pair_words[:, u : I // 2 : 2], identity[:])
+            vt_woven = sb.tile([P, P, PACK], BF16, name="vt_woven" + str(b), align_bytes=64)
+            nc.scalar.copy(out=vt_woven[:].bitcast(F32), in_=turned[:].rearrange("p u e -> p e u"))
+            return quantize(nc, sb, vt_woven[:], "vt" + str(b))
+
+        def finish(b, vt_q, bank, result_tag):
+            o_bank = psum.tile([P, J], F32, tag=bank)
+            multiply(nc, o_bank[:], vt_q, cols(0, P), gr1_q, cols(0, J))
+            result = sb.tile([P, J], F32, tag=result_tag)
+            nc.vector.tensor_tensor(result[:], o_bank[:], picked_memories[b][:], MULT)
+            nc.sync.dma_start(out=out[cols(b, P), :], in_=result[:])
+
+        vt0 = prepare(0, "bank_a")
+        vt1 = prepare(1, "bank_b")
+        finish(0, vt0, "bank_b", "result0")
+        finish(1, vt1, "bank_a", "result1")
+        vt2 = prepare(2, "bank_c")
+        vt3 = prepare(3, "bank_a")
+        finish(2, vt2, "bank_b", "val_block3")
+        finish(3, vt3, "bank_c", "result3")

@@ -25,8 +25,8 @@ M_HALVES = M // BANK
 J_HALVES = J // P
 
 
-def interleave(nc, woven, planes):
-    nc.vector.tensor_copy(
+def interleave(copy, woven, planes):
+    copy(
         out=woven.rearrange("p (c i) t -> p c t i", i=4),
         in_=planes.rearrange("p t (c i) -> p c t i", i=4),
     )
@@ -115,7 +115,7 @@ def tile_attend_tab_larger_gains_kernel(
             user_singles.append(single)
         val_blocks = []
         for b in range(E_BLOCKS):
-            block = sb.tile([P, T], F32, name="val_block" + str(b), tag="val_block" + str(b))
+            block = sb.tile([P, T], F32, name="val_block" + str(b), tag="val_block" + str(b), align_bytes=64)
             nc.sync.dma_start(out=block[:], in_=vals[cols(b, P), :])
             val_blocks.append(block)
 
@@ -123,12 +123,12 @@ def tile_attend_tab_larger_gains_kernel(
         make_identity(nc, identity[:])
 
         wm_woven = sb.tile([P, E, PACK], BF16, align_bytes=64)
-        interleave(nc, wm_woven[:], wm_raw[:])
+        interleave(nc.vector.tensor_copy, wm_woven[:], wm_raw[:])
         wm_q = quantize(nc, sb, wm_woven[:], "wm")
         memories = [sb.tile([P, M], F32, name="memories" + str(b)) for b in range(E_BLOCKS)]
         for h in range(M_HALVES):
             mstore_woven = sb.tile([P, BANK, PACK], BF16, name="mstore_woven" + str(h), align_bytes=64)
-            interleave(nc, mstore_woven[:], mstore_raw[h][:])
+            interleave(nc.vector.tensor_copy, mstore_woven[:], mstore_raw[h][:])
             mstore_q = quantize(nc, sb, mstore_woven[:], "mstore" + str(h))
             for b in range(E_BLOCKS):
                 memory_bank = psum.tile([P, BANK], F32, bufs=3)
@@ -151,7 +151,7 @@ def tile_attend_tab_larger_gains_kernel(
         keys_q = (picked_words, picked_scales)
 
         def table_half(columns_q, columns):
-            table_bank = psum.tile([P, PACK, P], F32, bufs=2)
+            table_bank = psum.tile([P, PACK, P], F32, tag="product_bank", bufs=2)
             for t in range(PACK):
                 multiply(nc, table_bank[:, t, :], keys_q, cols(t, P), columns_q, columns)
             return table_bank[:].rearrange("p t j -> p j t")
@@ -160,7 +160,7 @@ def tile_attend_tab_larger_gains_kernel(
         for t in range(PACK):
             nc.vector.tensor_copy(note_planes[:, t, :], note_pairs[t // 2][:, t % 2, :].indirect(note_list[:]))
         notes_woven = sb.tile([P, J, PACK], BF16, align_bytes=64)
-        interleave(nc, notes_woven[:], note_planes[:])
+        interleave(nc.vector.tensor_copy, notes_woven[:], note_planes[:])
         notes_q = quantize(nc, sb, notes_woven[:], "notes")
         g1 = sb.tile([P, J, PACK], F32)
         for h in range(J_HALVES):
@@ -173,8 +173,8 @@ def tile_attend_tab_larger_gains_kernel(
         nc.vector.tensor_copy(user_planes[:, 3, :P], user_singles[1][:].indirect(user_list[:, : P // 16]))
         nc.scalar.activation(user_planes[:, 3, P:], user_singles[1][:].indirect(user_list[:, P // 16 :]), COPY)
         users_woven = [sb.tile([P, P, PACK], BF16, name="users_woven" + str(h), align_bytes=64) for h in range(J_HALVES)]
-        for h in range(J_HALVES):
-            interleave(nc, users_woven[h][:], user_planes[:, :, cols(h, P)])
+        for h, copy in enumerate((nc.vector.tensor_copy, nc.scalar.copy)):
+            interleave(copy, users_woven[h][:], user_planes[:, :, cols(h, P)])
         users_q = [quantize(nc, sb, users_woven[h][:], "users" + str(h)) for h in range(J_HALVES)]
         g0 = sb.tile([P, J, PACK], F32)
         gr1 = sb.tile([P, J, PACK], BF16, align_bytes=64)
@@ -193,9 +193,9 @@ def tile_attend_tab_larger_gains_kernel(
 
         list_cols = I // 16
 
-        def prepare(b, bank):
+        def gather_and_turn(b):
             picked_vals = sb.tile([P, I], BF16, name="picked_vals" + str(b))
-            if b < E_BLOCKS - 1:
+            if b < 2:
                 nc.scalar.activation(picked_vals[:], val_blocks[b][:].indirect(token_list[:]), COPY)
             else:
                 nc.scalar.activation(
@@ -205,25 +205,34 @@ def tile_attend_tab_larger_gains_kernel(
                     picked_vals[:, I // 2 :], val_blocks[b][:].indirect(token_list[:, list_cols // 2 :])
                 )
             pair_words = picked_vals[:].bitcast(F32)
-            turned = psum.tile([P, 2, P], F32, tag=bank)
+            turned = psum.tile([P, 2, P], F32, bufs=2)
             for u in range(2):
                 nc.tensor.transpose(turned[:, u, :], pair_words[:, u : I // 2 : 2], identity[:])
-            vt_woven = sb.tile([P, P, PACK], BF16, name="vt_woven" + str(b), align_bytes=64)
-            nc.scalar.copy(out=vt_woven[:].bitcast(F32), in_=turned[:].rearrange("p u e -> p e u"))
-            return quantize(nc, sb, vt_woven[:], "vt" + str(b))
+            return turned
 
-        def finish(b, vt_q, bank, result_tag):
-            o_bank = psum.tile([P, J], F32, tag=bank)
+        def product(b, turned, vt_words):
+            nc.scalar.copy(out=vt_words.rearrange("p (e u) -> p e u", u=2), in_=turned[:].rearrange("p u e -> p e u"))
+            vt_q = quantize(nc, sb, vt_words.bitcast(BF16).rearrange("p (e t) -> p e t", t=PACK), "vt" + str(b))
+            o_bank = psum.tile([P, J], F32, tag="product_bank", bufs=2)
             multiply(nc, o_bank[:], vt_q, cols(0, P), gr1_q, cols(0, J))
-            result = sb.tile([P, J], F32, tag=result_tag)
-            nc.vector.tensor_tensor(result[:], o_bank[:], picked_memories[b][:], MULT)
-            nc.sync.dma_start(out=out[cols(b, P), :], in_=result[:])
+            return o_bank
 
-        vt0 = prepare(0, "bank_a")
-        vt1 = prepare(1, "bank_b")
-        finish(0, vt0, "bank_b", "result0")
-        finish(1, vt1, "bank_a", "result1")
-        vt2 = prepare(2, "bank_c")
-        vt3 = prepare(3, "bank_a")
-        finish(2, vt2, "bank_b", "val_block3")
-        finish(3, vt3, "bank_c", "result3")
+        def finish(b, o_bank, result):
+            nc.vector.tensor_tensor(result, o_bank[:], picked_memories[b][:], MULT)
+            nc.sync.dma_start(out=out[cols(b, P), :], in_=result)
+
+        own = [sb.tile([P, 2 * P], F32, name="own" + str(n), align_bytes=64) for n in range(3)]
+        turned0 = gather_and_turn(0)
+        turned1 = gather_and_turn(1)
+        after1 = sb.tile([P, J], F32, tag="val_block1", align_bytes=64)
+        o0 = product(0, turned0, after1[:])
+        turned2 = gather_and_turn(2)
+        after2 = sb.tile([P, 2 * J], F32, tag="val_block2", align_bytes=64)
+        finish(0, o0, after2[:, cols(0, J)])
+        o1 = product(1, turned1, after2[:, cols(1, J)])
+        o2 = product(2, turned2, own[0][:])
+        turned3 = gather_and_turn(3)
+        after3 = sb.tile([P, 2 * J], F32, tag="val_block3", align_bytes=64)
+        finish(1, o1, after3[:, cols(0, J)])
+        finish(2, o2, after3[:, cols(1, J)])
+        finish(3, product(3, turned3, own[1][:]), own[2][:])

@@ -21,7 +21,6 @@ P = 128
 PACK = 4
 BANK = 512
 E_BLOCKS = E // P
-M_HALVES = M // BANK
 J_HALVES = J // P
 
 
@@ -74,27 +73,22 @@ def tile_attend_tab_larger_gains_kernel(
             rows = src.rearrange("(p t) n -> p t n", t=PACK)
             pairs = []
             for a in range(2):
-                pair = sb.tile([P, 2, src.shape[1]], F32, name=name + str(a))
+                pair = sb.tile([P, 2, src.shape[1]], F32, name=name + str(a), align_bytes=256)
                 nc.sync.dma_start(out=pair[:], in_=rows[:, 2 * a : 2 * a + 2, :])
                 pairs.append(pair)
             return pairs
 
-        key_scales = sb.tile([P, T], U8)
+        key_scales = sb.tile([P, T], U8, align_bytes=256)
         nc.vector.memset(key_scales[:].bitcast(I32), 0)
-        wm_raw = sb.tile([P, PACK, E], F32)
+        wm_raw = sb.tile([P, PACK, E], F32, align_bytes=256)
         nc.sync.dma_start(out=wm_raw[:], in_=wm.rearrange("(p t) e -> p t e", t=PACK))
-        for q in range(4):
+        for r in range(4):
             nc.sync.dma_start(
-                out=key_scales[32 * q : 32 * q + 4, :].bitcast(I32),
-                in_=keys_scales[0, 4 * q : 4 * q + 4, :].bitcast(I32),
+                out=key_scales[r:P:32, :].bitcast(I32), in_=keys_scales[0, r:16:4, :].bitcast(I32)
             )
-        mstore_rows = mstore.rearrange("(p t) m -> p t m", t=PACK)
-        mstore_raw = []
-        for h in range(M_HALVES):
-            half = sb.tile([P, PACK, BANK], F32, name="mstore_raw" + str(h))
-            nc.sync.dma_start(out=half[:], in_=mstore_rows[:, :, cols(h, BANK)])
-            mstore_raw.append(half)
-        key_words = sb.tile([P, T], U32)
+        mstore_raw = sb.tile([P, PACK, M], F32, align_bytes=256)
+        nc.sync.dma_start(out=mstore_raw[:], in_=mstore.rearrange("(p t) m -> p t m", t=PACK))
+        key_words = sb.tile([P, T], U32, align_bytes=256)
         nc.sync.dma_start(
             out=key_words[:].bitcast(I32), in_=keys_words[0].rearrange("p n t -> p (n t)").bitcast(I32)
         )
@@ -106,16 +100,16 @@ def tile_attend_tab_larger_gains_kernel(
         nc.sync.dma_start(out=row_factors[:], in_=rowf.rearrange("(p t) o -> p (t o)", t=PACK))
         note_pairs = load_plane_pairs(notes, "note_pair")
         user_rows = users2.rearrange("(p t) n -> p t n", t=PACK)
-        user_pair = sb.tile([P, 2, Z], F32)
+        user_pair = sb.tile([P, 2, Z], F32, align_bytes=256)
         nc.sync.dma_start(out=user_pair[:], in_=user_rows[:, 0:2, :])
         user_singles = []
         for t in (2, 3):
-            single = sb.tile([P, Z], F32, name="user_single" + str(t))
+            single = sb.tile([P, Z], F32, name="user_single" + str(t), align_bytes=256)
             nc.sync.dma_start(out=single[:], in_=user_rows[:, t, :])
             user_singles.append(single)
         val_blocks = []
         for b in range(E_BLOCKS):
-            block = sb.tile([P, T], F32, name="val_block" + str(b), tag="val_block" + str(b), align_bytes=64)
+            block = sb.tile([P, T], F32, name="val_block" + str(b), tag="buffer" + str(b), align_bytes=256)
             nc.sync.dma_start(out=block[:], in_=vals[cols(b, P), :])
             val_blocks.append(block)
 
@@ -126,9 +120,9 @@ def tile_attend_tab_larger_gains_kernel(
         interleave(nc.vector.tensor_copy, wm_woven[:], wm_raw[:])
         wm_q = quantize(nc, sb, wm_woven[:], "wm")
         memories = [sb.tile([P, M], F32, name="memories" + str(b)) for b in range(E_BLOCKS)]
-        for h in range(M_HALVES):
+        for h, copy in enumerate((nc.vector.tensor_copy, nc.scalar.copy)):
             mstore_woven = sb.tile([P, BANK, PACK], BF16, name="mstore_woven" + str(h), align_bytes=64)
-            interleave(nc.vector.tensor_copy, mstore_woven[:], mstore_raw[h][:])
+            interleave(copy, mstore_woven[:], mstore_raw[:, :, cols(h, BANK)])
             mstore_q = quantize(nc, sb, mstore_woven[:], "mstore" + str(h))
             for b in range(E_BLOCKS):
                 memory_bank = psum.tile([P, BANK], F32, bufs=3)
@@ -139,6 +133,7 @@ def tile_attend_tab_larger_gains_kernel(
             picked = sb.tile([P, J], F32, name="picked_memories" + str(b))
             nc.scalar.activation(picked[:], memories[b][:].indirect(memory_list[:]), COPY)
             picked_memories.append(picked)
+
 
         picked_words = sb.tile([P, I], U32, align_bytes=64)
         nc.vector.tensor_copy(
@@ -210,29 +205,25 @@ def tile_attend_tab_larger_gains_kernel(
                 nc.tensor.transpose(turned[:, u, :], pair_words[:, u : I // 2 : 2], identity[:])
             return turned
 
-        def product(b, turned, vt_words):
-            nc.scalar.copy(out=vt_words.rearrange("p (e u) -> p e u", u=2), in_=turned[:].rearrange("p u e -> p e u"))
-            vt_q = quantize(nc, sb, vt_words.bitcast(BF16).rearrange("p (e t) -> p e t", t=PACK), "vt" + str(b))
+        def product(b, turned):
+            vt_woven = sb.tile([P, P, PACK], BF16, tag="buffer" + str(b + 1), align_bytes=256)
+            nc.scalar.copy(out=vt_woven[:].bitcast(F32), in_=turned[:].rearrange("p u e -> p e u"))
+            vt_q = quantize(nc, sb, vt_woven[:], "vt" + str(b))
             o_bank = psum.tile([P, J], F32, tag="product_bank", bufs=2)
             multiply(nc, o_bank[:], vt_q, cols(0, P), gr1_q, cols(0, J))
             return o_bank
 
-        def finish(b, o_bank, result):
-            nc.vector.tensor_tensor(result, o_bank[:], picked_memories[b][:], MULT)
-            nc.sync.dma_start(out=out[cols(b, P), :], in_=result)
+        def finish(b, o_bank):
+            result = sb.tile([P, J], F32, tag="buffer" + str(b + 2), align_bytes=256)
+            nc.vector.tensor_tensor(result[:], o_bank[:], picked_memories[b][:], MULT)
+            nc.sync.dma_start(out=out[cols(b, P), :], in_=result[:])
 
-        own = [sb.tile([P, 2 * P], F32, name="own" + str(n), align_bytes=64) for n in range(3)]
-        turned0 = gather_and_turn(0)
-        turned1 = gather_and_turn(1)
-        after1 = sb.tile([P, J], F32, tag="val_block1", align_bytes=64)
-        o0 = product(0, turned0, after1[:])
-        turned2 = gather_and_turn(2)
-        after2 = sb.tile([P, 2 * J], F32, tag="val_block2", align_bytes=64)
-        finish(0, o0, after2[:, cols(0, J)])
-        o1 = product(1, turned1, after2[:, cols(1, J)])
-        o2 = product(2, turned2, own[0][:])
-        turned3 = gather_and_turn(3)
-        after3 = sb.tile([P, 2 * J], F32, tag="val_block3", align_bytes=64)
-        finish(1, o1, after3[:, cols(0, J)])
-        finish(2, o2, after3[:, cols(1, J)])
-        finish(3, product(3, turned3, own[1][:]), own[2][:])
+        turned = [gather_and_turn(0)]
+        o_banks = []
+        for b in range(E_BLOCKS):
+            if b + 1 < E_BLOCKS:
+                turned.append(gather_and_turn(b + 1))
+            o_banks.append(product(b, turned[b]))
+            if b > 0:
+                finish(b - 1, o_banks[b - 1])
+        finish(E_BLOCKS - 1, o_banks[-1])

@@ -86,8 +86,12 @@ def tile_attend_tab_larger_gains_kernel(
             nc.sync.dma_start(
                 out=key_scales[r:P:32, :].bitcast(I32), in_=keys_scales[0, r:16:4, :].bitcast(I32)
             )
-        mstore_raw = sb.tile([P, PACK, M], F32, align_bytes=256)
-        nc.sync.dma_start(out=mstore_raw[:], in_=mstore.rearrange("(p t) m -> p t m", t=PACK))
+        mstore_rows = mstore.rearrange("(p t) m -> p t m", t=PACK)
+        mstore_raw = []
+        for h in range(M // BANK):
+            half = sb.tile([P, PACK, BANK], F32, name="mstore_raw" + str(h), align_bytes=256)
+            nc.sync.dma_start(out=half[:], in_=mstore_rows[:, :, cols(h, BANK)])
+            mstore_raw.append(half)
         key_words = sb.tile([P, T], U32, align_bytes=256)
         nc.sync.dma_start(
             out=key_words[:].bitcast(I32), in_=keys_words[0].rearrange("p n t -> p (n t)").bitcast(I32)
@@ -120,9 +124,9 @@ def tile_attend_tab_larger_gains_kernel(
         interleave(nc.vector.tensor_copy, wm_woven[:], wm_raw[:])
         wm_q = quantize(nc, sb, wm_woven[:], "wm")
         memories = [sb.tile([P, M], F32, name="memories" + str(b)) for b in range(E_BLOCKS)]
-        for h, copy in enumerate((nc.vector.tensor_copy, nc.scalar.copy)):
+        for h in range(M // BANK):
             mstore_woven = sb.tile([P, BANK, PACK], BF16, name="mstore_woven" + str(h), align_bytes=64)
-            interleave(copy, mstore_woven[:], mstore_raw[:, :, cols(h, BANK)])
+            interleave(nc.vector.tensor_copy, mstore_woven[:], mstore_raw[h][:])
             mstore_q = quantize(nc, sb, mstore_woven[:], "mstore" + str(h))
             for b in range(E_BLOCKS):
                 memory_bank = psum.tile([P, BANK], F32, bufs=3)
@@ -146,7 +150,7 @@ def tile_attend_tab_larger_gains_kernel(
         keys_q = (picked_words, picked_scales)
 
         def table_half(columns_q, columns):
-            table_bank = psum.tile([P, PACK, P], F32, tag="product_bank", bufs=2)
+            table_bank = psum.tile([P, PACK, P], F32, tag="product_bank", bufs=3)
             for t in range(PACK):
                 multiply(nc, table_bank[:, t, :], keys_q, cols(t, P), columns_q, columns)
             return table_bank[:].rearrange("p t j -> p j t")
@@ -209,14 +213,19 @@ def tile_attend_tab_larger_gains_kernel(
             vt_woven = sb.tile([P, P, PACK], BF16, tag="buffer" + str(b + 1), align_bytes=256)
             nc.scalar.copy(out=vt_woven[:].bitcast(F32), in_=turned[:].rearrange("p u e -> p e u"))
             vt_q = quantize(nc, sb, vt_woven[:], "vt" + str(b))
-            o_bank = psum.tile([P, J], F32, tag="product_bank", bufs=2)
-            multiply(nc, o_bank[:], vt_q, cols(0, P), gr1_q, cols(0, J))
-            return o_bank
+            width = J if b + 1 < E_BLOCKS else P
+            pieces = []
+            for n in range(J // width):
+                o_bank = psum.tile([P, width], F32, tag="product_bank", bufs=3)
+                multiply(nc, o_bank[:], vt_q, cols(0, P), gr1_q, cols(n, width))
+                pieces.append((cols(n, width), o_bank))
+            return pieces
 
-        def finish(b, o_bank):
+        def finish(b, pieces):
             result = sb.tile([P, J], F32, tag="buffer" + str(b + 2), align_bytes=256)
-            nc.vector.tensor_tensor(result[:], o_bank[:], picked_memories[b][:], MULT)
-            nc.sync.dma_start(out=out[cols(b, P), :], in_=result[:])
+            for j_cols, o_bank in pieces:
+                nc.vector.tensor_tensor(result[:, j_cols], o_bank[:], picked_memories[b][:, j_cols], MULT)
+                nc.sync.dma_start(out=out[cols(b, P), j_cols], in_=result[:, j_cols])
 
         turned = [gather_and_turn(0)]
         o_banks = []

from contextlib import ExitStack

import concourse.mybir as mybir
from concourse.masks import make_identity

D, T, I, J, U, Z, E, M, C = 512, 2048, 512, 256, 1024, 1024, 512, 1024, 512
FLOPS = 2 * (2 * D * I * J + I * E * J + C * E * M)

F32 = mybir.dt.float32
BF16 = mybir.dt.bfloat16
I32 = mybir.dt.int32
U32 = mybir.dt.uint32
U16 = mybir.dt.uint16
U8 = mybir.dt.uint8
FP8X4 = mybir.dt.float8_e4m3fn_x4
COPY = mybir.ActivationFunctionType.Copy
MULT = mybir.AluOpType.mult
MAX = mybir.AluOpType.max

P = 128
PACK = 4
BANK = 512
E_BLOCKS = E // P
J_HALVES = J // P


def interleave(copy, woven, planes):
    copy(
        out=woven.rearrange("p (c i) t -> p c t i", i=4),
        in_=planes.rearrange("p t (c i) -> p c t i", i=4),
    )


def quantize(nc, pool, woven, name):
    width = woven.shape[1]
    codes = pool.tile([P, width], U32, name=name + "_codes", align_bytes=64)
    scales = pool.tile([P, width], U8, name=name + "_scales", align_bytes=64)
    nc.vector.quantize_mx(out=codes[:].bitcast(FP8X4), scales=scales[:], in_=woven.rearrange("p w t -> p (w t)"))
    return codes, scales


def multiply(nc, out, left, left_cols, right, right_cols):
    nc.tensor.matmul_mx(
        out=out,
        lhsT=left[0][:, left_cols].bitcast(FP8X4),
        lhsT_scale=left[1][:, left_cols],
        rhs=right[0][:, right_cols].bitcast(FP8X4),
        rhs_scale=right[1][:, right_cols],
        start=True,
        stop=True,
    )


def cols(n, width):
    return slice(n * width, (n + 1) * width)


def tile_attend_tab_larger_gains_kernel(
    tc, keys_words, keys_scales, notes, users2, rowf, vals, wm, mstore, offs, offs2, offs3, offs4, out
):
    nc = tc.nc
    with ExitStack() as ctx:
        lists = ctx.enter_context(tc.tile_pool(name="lists", bufs=1))
        sb = ctx.enter_context(tc.tile_pool(name="sb", bufs=1))
        psum = ctx.enter_context(tc.psum_pool(name="psum", bufs=1))

        def load_list(src, name):
            tile = lists.tile(list(src.shape), U16, name=name)
            nc.sync.dma_start(tile[:], src)
            return tile

        def load_plane_pairs(src, name):
            rows = src.rearrange("(p t) n -> p t n", t=PACK)
            pairs = []
            for a in range(2):
                pair = sb.tile([P, 2, src.shape[1]], F32, name=name + str(a), align_bytes=256)
                nc.sync.dma_start(out=pair[:], in_=rows[:, 2 * a : 2 * a + 2, :])
                pairs.append(pair)
            return pairs

        key_scales = sb.tile([P, T], U8, align_bytes=256)
        nc.vector.memset(key_scales[:].bitcast(I32), 0)
        wm_raw = sb.tile([P, PACK, E], F32, align_bytes=256)
        nc.sync.dma_start(out=wm_raw[:], in_=wm.rearrange("(p t) e -> p t e", t=PACK))
        for r in range(4):
            nc.sync.dma_start(
                out=key_scales[r:P:32, :].bitcast(I32), in_=keys_scales[0, r:16:4, :].bitcast(I32)
            )
        mstore_rows = mstore.rearrange("(p t) m -> p t m", t=PACK)
        mstore_raw = []
        for h in range(M // BANK):
            half = sb.tile([P, PACK, BANK], F32, name="mstore_raw" + str(h), align_bytes=256)
            nc.sync.dma_start(out=half[:], in_=mstore_rows[:, :, cols(h, BANK)])
            mstore_raw.append(half)
        key_words = sb.tile([P, T], U32, align_bytes=256)
        nc.sync.dma_start(
            out=key_words[:].bitcast(I32), in_=keys_words[0].rearrange("p n t -> p (n t)").bitcast(I32)
        )
        token_list = load_list(offs, "token_list")
        memory_list = load_list(offs4, "memory_list")
        note_list = load_list(offs2, "note_list")
        user_list = load_list(offs3, "user_list")
        row_factors = sb.tile([P, PACK], F32)
        nc.sync.dma_start(out=row_factors[:], in_=rowf.rearrange("(p t) o -> p (t o)", t=PACK))
        note_pairs = load_plane_pairs(notes, "note_pair")
        user_rows = users2.rearrange("(p t) n -> p t n", t=PACK)
        user_pair = sb.tile([P, 2, Z], F32, align_bytes=256)
        nc.sync.dma_start(out=user_pair[:], in_=user_rows[:, 0:2, :])
        user_singles = []
        for t in (2, 3):
            single = sb.tile([P, Z], F32, name="user_single" + str(t), align_bytes=256)
            nc.sync.dma_start(out=single[:], in_=user_rows[:, t, :])
            user_singles.append(single)
        val_blocks = []
        for b in range(E_BLOCKS):
            block = sb.tile([P, T], F32, name="val_block" + str(b), tag="buffer" + str(b), align_bytes=256)
            nc.sync.dma_start(out=block[:], in_=vals[cols(b, P), :])
            val_blocks.append(block)

        identity = sb.tile([P, P], F32)
        make_identity(nc, identity[:])

        wm_woven = sb.tile([P, E, PACK], BF16, align_bytes=64)
        interleave(nc.vector.tensor_copy, wm_woven[:], wm_raw[:])
        wm_q = quantize(nc, sb, wm_woven[:], "wm")
        memories = [sb.tile([P, M], F32, name="memories" + str(b)) for b in range(E_BLOCKS)]
        for h in range(M // BANK):
            mstore_woven = sb.tile([P, BANK, PACK], BF16, name="mstore_woven" + str(h), align_bytes=64)
            interleave(nc.vector.tensor_copy, mstore_woven[:], mstore_raw[h][:])
            mstore_q = quantize(nc, sb, mstore_woven[:], "mstore" + str(h))
            for b in range(E_BLOCKS):
                memory_bank = psum.tile([P, BANK], F32, bufs=3)
                multiply(nc, memory_bank[:], wm_q, cols(b, P), mstore_q, cols(0, BANK))
                nc.scalar.copy(out=memories[b][:, cols(h, BANK)], in_=memory_bank[:])
        picked_memories = []
        for b in range(E_BLOCKS):
            picked = sb.tile([P, J], F32, name="picked_memories" + str(b))
            nc.scalar.activation(picked[:], memories[b][:].indirect(memory_list[:]), COPY)
            picked_memories.append(picked)


        picked_words = sb.tile([P, I], U32, align_bytes=64)
        nc.vector.tensor_copy(
            picked_words[:].rearrange("p (t s) -> p s t", t=PACK), key_words[:].indirect(token_list[:])
        )
        picked_scales = sb.tile([P, I], U8, align_bytes=64)
        nc.vector.tensor_copy(
            picked_scales[:].rearrange("p (t s) -> p s t", t=PACK), key_scales[:].indirect(token_list[:])
        )
        keys_q = (picked_words, picked_scales)

        def table_half(columns_q, columns):
            table_bank = psum.tile([P, PACK, P], F32, tag="product_bank", bufs=3)
            for t in range(PACK):
                multiply(nc, table_bank[:, t, :], keys_q, cols(t, P), columns_q, columns)
            return table_bank[:].rearrange("p t j -> p j t")

        note_planes = sb.tile([P, PACK, J], F32)
        for t in range(PACK):
            nc.vector.tensor_copy(note_planes[:, t, :], note_pairs[t // 2][:, t % 2, :].indirect(note_list[:]))
        notes_woven = sb.tile([P, J, PACK], BF16, align_bytes=64)
        interleave(nc.vector.tensor_copy, notes_woven[:], note_planes[:])
        notes_q = quantize(nc, sb, notes_woven[:], "notes")
        g1 = sb.tile([P, J, PACK], F32)
        for h in range(J_HALVES):
            nc.scalar.copy(out=g1[:, cols(h, P), :], in_=table_half(notes_q, cols(h, P)))

        user_planes = sb.tile([P, PACK, J], F32)
        nc.vector.tensor_copy(user_planes[:, 0, :], user_pair[:, 0, :].indirect(user_list[:]))
        nc.scalar.activation(user_planes[:, 1, :], user_pair[:, 1, :].indirect(user_list[:]), COPY)
        nc.vector.tensor_copy(user_planes[:, 2, :], user_singles[0][:].indirect(user_list[:]))
        nc.vector.tensor_copy(user_planes[:, 3, :P], user_singles[1][:].indirect(user_list[:, : P // 16]))
        nc.scalar.activation(user_planes[:, 3, P:], user_singles[1][:].indirect(user_list[:, P // 16 :]), COPY)
        users_woven = [sb.tile([P, P, PACK], BF16, name="users_woven" + str(h), align_bytes=64) for h in range(J_HALVES)]
        for h, copy in enumerate((nc.vector.tensor_copy, nc.scalar.copy)):
            interleave(copy, users_woven[h][:], user_planes[:, :, cols(h, P)])
        users_q = [quantize(nc, sb, users_woven[h][:], "users" + str(h)) for h in range(J_HALVES)]
        g0 = sb.tile([P, J, PACK], F32)
        gr1 = sb.tile([P, J, PACK], BF16, align_bytes=64)
        for h in range(J_HALVES):
            nc.vector.tensor_tensor(
                g0[:, cols(h, P), :], table_half(users_q[h], cols(0, P)), g1[:, cols(h, P), :], MAX
            )
        for h in range(J_HALVES):
            nc.vector.tensor_tensor(
                gr1[:, cols(h, P), :],
                g0[:, cols(h, P), :],
                row_factors[:].unsqueeze(1).to_broadcast([P, P, PACK]),
                MULT,
            )
        gr1_q = quantize(nc, sb, gr1[:], "gr1")

        list_cols = I // 16

        def gather_and_turn(b):
            picked_vals = sb.tile([P, I], BF16, name="picked_vals" + str(b))
            if b < 2:
                nc.scalar.activation(picked_vals[:], val_blocks[b][:].indirect(token_list[:]), COPY)
            else:
                nc.scalar.activation(
                    picked_vals[:, : I // 2], val_blocks[b][:].indirect(token_list[:, : list_cols // 2]), COPY
                )
                nc.vector.tensor_copy(
                    picked_vals[:, I // 2 :], val_blocks[b][:].indirect(token_list[:, list_cols // 2 :])
                )
            pair_words = picked_vals[:].bitcast(F32)
            turned = psum.tile([P, 2, P], F32, bufs=2)
            for u in range(2):
                nc.tensor.transpose(turned[:, u, :], pair_words[:, u : I // 2 : 2], identity[:])
            return turned

        def product(b, turned):
            vt_woven = sb.tile([P, P, PACK], BF16, tag="buffer" + str(b + 1), align_bytes=256)
            nc.scalar.copy(out=vt_woven[:].bitcast(F32), in_=turned[:].rearrange("p u e -> p e u"))
            vt_q = quantize(nc, sb, vt_woven[:], "vt" + str(b))
            width = J if b + 1 < E_BLOCKS else P
            pieces = []
            for n in range(J // width):
                o_bank = psum.tile([P, width], F32, tag="product_bank", bufs=3)
                multiply(nc, o_bank[:], vt_q, cols(0, P), gr1_q, cols(n, width))
                pieces.append((cols(n, width), o_bank))
            return pieces

        def finish(b, pieces):
            result = sb.tile([P, J], F32, tag="buffer" + str(b + 2), align_bytes=256)
            for j_cols, o_bank in pieces:
                nc.vector.tensor_tensor(result[:, j_cols], o_bank[:], picked_memories[b][:, j_cols], MULT)
                nc.sync.dma_start(out=out[cols(b, P), j_cols], in_=result[:, j_cols])

        turned = [gather_and_turn(0)]
        o_banks = []
        for b in range(E_BLOCKS):
            if b + 1 < E_BLOCKS:
                turned.append(gather_and_turn(b + 1))
            o_banks.append(product(b, turned[b]))
            if b > 0:
                finish(b - 1, o_banks[b - 1])
        finish(E_BLOCKS - 1, o_banks[-1])
